import numpy as np
import ml_dtypes


def mxq(x, axis, fmt="e4m3"):
    dtype, down = {"e4m3": (ml_dtypes.float8_e4m3fn, 7), "e5m2": (ml_dtypes.float8_e5m2, 14)}[fmt]
    v = np.moveaxis(np.asarray(x, np.float32).astype(ml_dtypes.bfloat16).astype(np.float64), axis, -1)
    blocks = v.reshape(v.shape[:-1] + (-1, 32))
    amax = np.abs(blocks).max(-1, keepdims=True)
    byte = np.maximum(np.where(amax > 0, np.frexp(amax)[1] - 1 + 127, 0) - down, 1)
    scale = np.exp2(byte - 127.0)
    codes = (blocks / scale).astype(np.float32).astype(dtype).astype(np.float64)
    return np.moveaxis((codes * scale).reshape(v.shape), -1, axis)


WIDE = False


def mx_kscale(k):
    if not WIDE:
        return np.ones(k)
    levels = np.array([10, -10, 5, -5, 0])
    if k % 512:
        return np.exp2(np.random.permutation(np.resize(levels, k // 32))).repeat(32)
    a = np.empty((k // 512, 16))
    for p in range(k // 512):
        a[p, :8] = np.random.permutation(np.resize(levels, 8))
        for g in range(8):
            far = levels[np.abs(levels - a[p, g]) >= 10]
            a[p, g + 8] = far[np.random.randint(len(far))]
    return np.exp2(a.ravel()).repeat(32)


BF16 = ml_dtypes.bfloat16


def bf(x):
    return np.asarray(x, np.float32).astype(BF16)


def f64(x):
    return np.asarray(x).astype(np.float64)


E2M1 = np.array([0.0, 0.5, 1.0, 1.5, 2.0, 3.0, 4.0, 6.0, -0.0, -0.5, -1.0, -1.5, -2.0, -3.0, -4.0, -6.0])


def pack_weight(w, fmt):
    k, n = w.shape
    w = f64(bf(w)).reshape(k // 32, 32, n)
    amax = np.abs(w).max(1)
    if fmt == "e4m3":
        byte = np.frexp(amax)[1] - 1 + 127 - 7
    else:
        mant, ex = np.frexp(amax / 6.0)
        byte = np.where(mant > 0.5, ex, ex - 1) + 127
    byte = np.clip(np.where(amax > 0, byte, 1), 1, 254)
    scaled = (w * np.exp2(127.0 - byte)[:, None, :]).reshape(k, n).astype(np.float32)
    by_word = np.ascontiguousarray(scaled.reshape(k // 512, 128, 4, n).transpose(0, 1, 3, 2))
    if fmt == "e4m3":
        words = by_word.astype(ml_dtypes.float8_e4m3fn).view(np.uint8)
    else:
        c = by_word.astype(ml_dtypes.float4_e2m1fn).view(np.uint8) & 0xF
        words = c[..., 0::2] | (c[..., 1::2] << 4)
    return np.ascontiguousarray(words), np.ascontiguousarray(byte.astype(np.uint8).reshape(k // 512, 16, n))


def unpack_weight(words, scales, fmt):
    g, p, n, _ = words.shape
    if fmt == "e4m3":
        vals = np.ascontiguousarray(words).view(ml_dtypes.float8_e4m3fn).astype(np.float64)
    else:
        nib = np.empty((g, p, n, 4), np.uint8)
        nib[..., 0::2] = words & 0xF
        nib[..., 1::2] = words >> 4
        vals = E2M1[nib]
    vals = vals * np.repeat(np.exp2(scales.astype(np.float64) - 127.0), 8, axis=1)[..., None]
    return vals.transpose(0, 1, 3, 2).reshape(g * 512, n)

E4M3FN = np.array([(-1.0 if i & 128 else 1.0) * ((1.0 + (i & 7) / 8.0) * 2.0 ** (((i >> 3) & 15) - 7) if i & 120 else (i & 7) * 2.0 ** -9) for i in range(256)])


def e4m3fn_bytes(y):
    return np.clip(np.asarray(y, np.float64), -448.0, 448.0).astype(np.float32).astype(ml_dtypes.float8_e4m3fn).view(np.uint8)


def e4m3fn_values(b):
    return E4M3FN[b]


T, D, F = 2048, 1024, 1024


def erf(u):
    c = np.clip(u, -6.0, 6.0)
    q = 2.0 * c * c
    term = np.array(c)
    total = np.array(c)
    for n in range(1, 151):
        term *= q / (2 * n + 1)
        total += term
    return np.where(np.abs(u) > 6.0, np.sign(u), 2.0 / np.sqrt(np.pi) * np.exp(-c * c) * total)


def gelu_erf_grad(a):
    cdf = 0.5 * (1.0 + erf(a / np.sqrt(2.0)))
    pdf_term = a * np.exp(-np.square(a) / 2.0) / np.sqrt(2.0 * np.pi)
    return cdf + pdf_term


def frobenius(z):
    return np.sqrt(np.sum(np.square(z), axis=(0, 1)))


def draw0():
    s, t = mx_kscale(D), mx_kscale(T)
    x = bf(np.random.standard_normal((T, D)) / t[:, None])
    a = bf(np.random.standard_normal((T, F)))
    dy = bf(np.random.standard_normal((T, D)) * s[None, :] * t[:, None])
    w2_words, w2_scales = pack_weight((np.random.standard_normal((F, D)) / np.sqrt(D) / s[None, :]).T, "e4m3")
    return {
        "x": x,
        "a": a,
        "dy": dy,
        "w2_words": w2_words,
        "w2_scales": w2_scales,
        "w1": bf(np.random.standard_normal((D, F))),
        "m": bf(np.random.standard_normal((D, F)) * 0.3),
        "v": bf(np.random.uniform(0.2, 1.0, (D, F))),
    }


def core(x, a, dy, w2_words, w2_scales, w1, m, v):
    x, a, dy, w1, m, v = f64(x), f64(a), f64(dy), f64(w1), f64(m), f64(v)
    tokens = x.shape[0]
    dh = mxq(dy, 1, "e4m3") @ unpack_weight(w2_words, w2_scales, "e4m3")
    da = dh * gelu_erf_grad(a)
    g = (mxq(x, 0, "e4m3").T @ mxq(da, 0, "e4m3")) / np.sqrt(tokens)
    m_new = 0.6 * m + 0.4 * g
    v_new = 0.6 * v + 0.4 * np.square(g)
    r = m_new / np.sqrt(v_new) + 0.1 * w1
    trust = frobenius(w1) / frobenius(r)
    return w1 - 0.5 * trust * r


def setup_inputs():
    drawn = draw0()
    full = np.asarray(drawn['x']).astype(np.float64)
    scale = (np.abs(full).reshape(16, 128, 8, 128).max(axis=(1, 3)) / 448.0).astype(np.float32)
    given = {}
    for key, value in drawn.items():
        if key == 'x':
            given['x_bytes'] = e4m3fn_bytes(full / np.repeat(np.repeat(scale.astype(np.float64), 128, axis=0), 128, axis=1))
            given['x_scale'] = scale
        else:
            given[key] = value
    return given


def reference(x_bytes, x_scale, a, dy, w2_words, w2_scales, w1, m, v):
    return core(e4m3fn_values(x_bytes) * np.repeat(np.repeat(x_scale.astype(np.float64), 128, axis=0), 128, axis=1), a, dy, w2_words, w2_scales, w1, m, v)

import math
from contextlib import ExitStack

import concourse.mybir as mybir
from concourse.masks import make_identity

T, D, F = 2048, 1024, 1024
FLOPS = 2 * T * D * F * 2

F32 = mybir.dt.float32
BF16 = mybir.dt.bfloat16
I32 = mybir.dt.int32
U32 = mybir.dt.uint32
U8 = mybir.dt.uint8
FP8 = mybir.dt.float8_e4m3fn
FP8X4 = mybir.dt.float8_e4m3fn_x4
ACT = mybir.ActivationFunctionType
ALU = mybir.AluOpType

P = 128
PACK = 4
GROUPS = T // (P * PACK)
CHUNKS = 4
CW = F // CHUNKS
UNITS = CHUNKS * GROUPS
PAIRS = 4

SHIFT = 1e-12
LOG_PDF = -0.5 * math.log(2.0 * math.pi)
G_INTO_M = (0.4 / 0.6) / math.sqrt(T)
G_INTO_V = math.sqrt((0.4 / 0.6) / T)
V_SCALE = 1.0 / 60.0

WORK_TILES = 23
A_TILES = 10
SQUARE_ON_VECTOR = ()


def tile_lambmlpbackwardstep_d2p_kernel(tc, x_bytes, x_scale, a, dy, w2_words, w2_scales, w1, m, v, out):
    nc = tc.nc
    with ExitStack() as ctx:
        keep = ctx.enter_context(tc.tile_pool(name="keep", bufs=1))
        psum = ctx.enter_context(tc.psum_pool(name="psum", bufs=1))
        ctx.enter_context(
            tc.manual_schedule(engines={mybir.EngineType.SP, mybir.EngineType.Activation})
        )

        ident_bf = keep.tile([P, P], BF16, name="ident_bf")
        ident = keep.tile([P, P], F32, name="ident")
        ones = keep.tile([P, P], F32, name="ones")
        w_words = keep.tile([P, 2, F], U32, name="w_words", align_bytes=64)
        w_scales = keep.tile([P, 2, F], U8, name="w_scales", align_bytes=64)
        dy_codes = [keep.tile([P, 2, 2, P], U32, name="dy_codes%d" % i, align_bytes=64) for i in range(2 * GROUPS)]
        dy_scales = [keep.tile([P, 2, 2, P], U8, name="dy_scales%d" % i, align_bytes=64) for i in range(2 * GROUPS)]
        x_codes = [keep.tile([P, D // 2], U32, name="x_codes%d" % i, align_bytes=64) for i in range(2 * GROUPS)]
        x_scales = [keep.tile([P, D // 2], U8, name="x_scales%d" % i, align_bytes=64) for i in range(2 * GROUPS)]
        da_codes = [keep.tile([P, CW], U32, name="da_codes%d" % i, align_bytes=64) for i in range(2 * GROUPS)]
        da_scales = [keep.tile([P, CW], U8, name="da_scales%d" % i, align_bytes=64) for i in range(2 * GROUPS)]
        block_scale = keep.tile([P, 104], F32, name="block_scale")
        a_tiles = [keep.tile([P, PACK, CW], BF16, name="a_tile%d" % i) for i in range(A_TILES)]
        slope = [keep.tile([P, 2, P, PACK], F32, name="slope%d" % i) for i in range(2)]
        da_tiles = [keep.tile([P, 2, P, PACK], BF16, name="da_tile%d" % i, align_bytes=64) for i in range(2)]
        work = [keep.tile([P, 1024], F32, name="work%d" % i) for i in range(WORK_TILES)]
        r_sums = keep.tile([P, UNITS], F32, name="r_sums")
        r_sum = keep.tile([P, 1], F32, name="r_sum")
        w_sum = keep.tile([P, 1], F32, name="w_sum")
        w_inv = keep.tile([P, 1], F32, name="w_inv")
        kappa = keep.tile([P, 1], F32, name="kappa")
        keep_w = keep.tile([P, 1], F32, name="keep_w")
        minus_kappa = keep.tile([P, 1], F32, name="minus_kappa")
        a_banks = [psum.tile([P, 2, PACK, P], BF16, name="a_bank%d" % i) for i in range(2)]
        sum_banks = [psum.tile([P, PACK, P], F32, name="sum_bank%d" % i) for i in range(2)]
        dh_banks = [psum.tile([P, PACK, P], F32, name="dh_bank%d" % i) for i in range(2)]
        acc_banks = [psum.tile([P, PACK, P], F32, name="acc_bank%d" % i) for i in range(2)]
        head_banks = acc_banks + sum_banks + dh_banks

        late = {}
        free = {"work": list(range(WORK_TILES)), "acc": [0, 1]}
        held = {}
        turn = {"a_bank": 0}

        def take(kind, key):
            slot = free[kind][0]
            free[kind].remove(slot)
            held[key] = (kind, slot)

        def give(key):
            kind, slot = held[key]
            free[kind].append(slot)

        def tile_of(key):
            kind, slot = held[key]
            return {"work": work, "acc": acc_banks}[kind][slot]

        make_identity(nc, ident_bf[:])
        make_identity(nc, ident[:])
        nc.gpsimd.memset(w_scales[:].rearrange("p h n -> p (h n)").bitcast(U32), 0)
        nc.gpsimd.memset(ones[:], 1.0)

        def load_a(u):
            c, g = divmod(u, GROUPS)
            rows = a[g * 512 : (g + 1) * 512, c * CW : (c + 1) * CW]
            nc.sync.dma_start(out=a_tiles[u % A_TILES][:], in_=rows.rearrange("(p t) f -> p t f", t=PACK))

        def load_dy(i):
            g, half = divmod(i, 2)
            rows = dy[g * 512 : (g + 1) * 512, :].rearrange("(p t) k -> p t k", t=PACK)
            nc.sync.dma_start(out=late["dy_raw"][i % 4][:], in_=rows[:, 2 * half : 2 * half + 2, :])

        def load_x(g):
            rows = x_bytes[g * 512 : (g + 1) * 512, :].rearrange("(p t) d -> p (t d)", t=PACK)
            nc.sync.dma_start(out=late["x_raw"][g % 2][:], in_=rows)

        def load_block_scales():
            flat = x_scale.rearrange("i j -> (i j)")
            for q in range(4):
                nc.sync.dma_start(
                    out=block_scale[32 * q : 32 * q + 32, :], in_=flat[8 * q : 8 * q + 104].partition_broadcast(32)
                )

        def load_w2():
            for q in range(4):
                nc.sync.dma_start(
                    out=w_scales[32 * q : 32 * q + 4, :, :].bitcast(I32),
                    in_=w2_scales[:, 4 * q : 4 * q + 4, :].rearrange("h r n -> r h n").bitcast(I32),
                )
            nc.sync.dma_start(
                out=w_words[:].bitcast(I32), in_=w2_words.rearrange("h p n t -> p h (n t)").bitcast(I32)
            )

        def load_moments(i):
            c, half = divmod(i, 2)
            for src, name in ((m, "m"), (v, "v")):
                rows = src.rearrange("(i p) f -> p i f", p=P)[:, 4 * half : 4 * half + 4, c * CW : (c + 1) * CW]
                nc.sync.dma_start(out=late[name][i % 2][:], in_=rows)

        def load_w1(half):
            rows = w1.rearrange("(i p) f -> p i f", p=P)[:, 4 * half : 4 * half + 4, :]
            nc.sync.dma_start(out=late["w1"][half][:], in_=rows)

        def w1_rows(i):
            return late["w1"][i // 4][:, i % 4, :]

        def turn_dy(i, tt):
            bank = head_banks[(2 * i + tt) % 6]
            words = late["dy_raw"][i % 4][:, tt, :].bitcast(F32)
            for h in range(2):
                for u in range(2):
                    nc.tensor.transpose(bank[:, 2 * h + u, :], words[:, 256 * h + u : 256 * (h + 1) : 2], ident[:])
            nc.vector.tensor_copy(
                out=late["dy_t"][i % 2][:, tt, :, :, :], in_=bank[:].rearrange("p (h u) r -> p h r u", u=2)
            )

        def quantize_dy(i):
            nc.vector.quantize_mx(
                out=dy_codes[i][:].rearrange("p t h r -> p (t h r)").bitcast(FP8X4),
                scales=dy_scales[i][:].rearrange("p t h r -> p (t h r)"),
                in_=late["dy_t"][i % 2][:].rearrange("p t h r u -> p (t h r u)").bitcast(BF16),
            )

        def widen_x(g):
            nc.vector.tensor_copy(
                out=late["x_wide"][:].rearrange("p t d -> p (t d)"), in_=late["x_raw"][g % 2][:].bitcast(FP8)
            )

        def scale_x(g, j):
            dst = late["x_packed"][j // 4][:, (j % 4) * P : (j % 4 + 1) * P, :]
            src = late["x_wide"][:, :, j * P : (j + 1) * P]
            nc.vector.tensor_scalar(
                out=dst.rearrange("p (c i) t -> p c t i", i=4),
                in0=src.rearrange("p t (c i) -> p c t i", i=4),
                scalar1=block_scale[:, 32 * g + j : 32 * g + j + 1],
                scalar2=None,
                op0=ALU.mult,
            )

        def quantize_x(g, half):
            nc.vector.quantize_mx(
                out=x_codes[2 * g + half][:].bitcast(FP8X4),
                scales=x_scales[2 * g + half][:],
                in_=late["x_packed"][half][:].rearrange("p d t -> p (d t)"),
            )

        def turn_a(u):
            bank = a_banks[turn["a_bank"] % 2]
            turn["a_bank"] = turn["a_bank"] + 1
            for fb in range(2):
                for t in range(PACK):
                    nc.tensor.transpose(bank[:, fb, t, :], a_tiles[u % A_TILES][:, t, fb * P : (fb + 1) * P], ident_bf[:])
            return bank[:].rearrange("p b t r -> p (b t r)")

        def from_a(u, names):
            turned = turn_a(u)
            for name in names:
                take("work", (name, u))
                func = {"gelu": ACT.Gelu, "square": ACT.Square}[name]
                nc.scalar.activation(out=tile_of((name, u))[:], in_=turned, func=func, bias=SHIFT)

        def density(u):
            take("work", ("pdf", u))
            nc.scalar.activation(
                out=tile_of(("pdf", u))[:], in_=tile_of(("square", u))[:], func=ACT.Exp, scale=-0.5, bias=LOG_PDF
            )

        def inverse_abs(u, in_place):
            if in_place:
                held[("inv", u)] = held[("square", u)]
            else:
                take("work", ("inv", u))
            nc.scalar.activation(out=tile_of(("inv", u))[:], in_=tile_of(("square", u))[:], func=ACT.Abs_reciprocal_sqrt)

        def density_in_place(u):
            held[("pdf", u)] = held[("square", u)]
            nc.scalar.activation(
                out=tile_of(("pdf", u))[:], in_=tile_of(("square", u))[:], func=ACT.Exp, scale=-0.5, bias=LOG_PDF
            )

        def inverse_square(u):
            nc.scalar.activation(out=tile_of(("inv", u))[:], in_=tile_of(("inv", u))[:], func=ACT.Square)

        def cdf_term(u, last):
            gelu = tile_of(("gelu", u))
            nc.vector.tensor_tensor(out=gelu[:], in0=gelu[:], in1=tile_of(("inv", u))[:], op=ALU.mult)
            if last:
                give(("inv", u))

        def make_slope(u, fb):
            bank = sum_banks[fb]
            for t in range(PACK):
                cols = slice((fb * PACK + t) * P, (fb * PACK + t + 1) * P)
                for name in ("gelu", "pdf"):
                    nc.tensor.matmul(
                        bank[:, t, :],
                        lhsT=tile_of((name, u))[:, cols],
                        rhs=ident[:],
                        is_transpose=True,
                        start=name == "gelu",
                        stop=name == "pdf",
                    )
            if fb == 1:
                give(("gelu", u))
                give(("pdf", u))
            nc.vector.scalar_tensor_tensor(
                out=slope[u % 2][:, fb, :, :],
                in0=a_tiles[u % A_TILES][:, :, fb * P : (fb + 1) * P].rearrange("p t f -> p f t"),
                scalar=SHIFT,
                in1=bank[:].rearrange("p t f -> p f t"),
                op0=ALU.add,
                op1=ALU.mult,
            )

        def make_da(u, fb):
            c, g = divmod(u, GROUPS)
            bank = dh_banks[fb]
            cols = slice(c * CW + fb * P, c * CW + (fb + 1) * P)
            for t in range(PACK):
                i, tt = 2 * g + t // 2, t % 2
                for h in range(2):
                    nc.tensor.matmul_mx(
                        out=bank[:, t, :],
                        lhsT=dy_codes[i][:, tt, h, :].bitcast(FP8X4),
                        lhsT_scale=dy_scales[i][:, tt, h, :],
                        rhs=w_words[:, h, cols].bitcast(FP8X4),
                        rhs_scale=w_scales[:, h, cols],
                        start=h == 0,
                        stop=h == 1,
                    )
            nc.vector.tensor_tensor(
                out=da_tiles[u % 2][:, fb, :, :],
                in0=bank[:].rearrange("p t f -> p f t"),
                in1=slope[u % 2][:, fb, :, :],
                op=ALU.mult,
            )

        def quantize_da(u):
            nc.vector.quantize_mx(
                out=da_codes[u % 8][:].bitcast(FP8X4),
                scales=da_scales[u % 8][:],
                in_=da_tiles[u % 2][:].rearrange("p b f t -> p (b f t)"),
            )

        def update_tile(c, j):
            if c < 2:
                whole = late["update"][j][:]
            else:
                whole = tile_of(("update", j))[:].rearrange("p (i f) -> p i f", i=2)
            return whole

        def update_view(c, j):
            return update_tile(c, j)[:, :, (c % 2) * CW : (c % 2 + 1) * CW]

        def grad_view(c, j):
            return tile_of(("grad", c, j))[:].rearrange("p (i b) f -> p i (b f)", i=2)

        def second_view(c, j):
            return tile_of(("second", c, j // 2))[:].rearrange("p (j i f) -> p j i f", j=2, i=2)[:, j % 2, :, :]

        def moment_view(name, c, j):
            return late[name][j // 2][:, 2 * (j % 2) : 2 * (j % 2) + 2, :]

        def first_moment(c, j):
            take("acc", ("grad", c, j))
            if c == 2:
                take("work", ("update", j))
            grad = grad_view(c, j)
            for di in range(2):
                i = 2 * j + di
                for g in range(GROUPS):
                    cols = slice((i % 4) * P, (i % 4 + 1) * P)
                    nc.tensor.matmul_mx(
                        out=grad[:, di, :],
                        lhsT=x_codes[2 * g + i // 4][:, cols].bitcast(FP8X4),
                        lhsT_scale=x_scales[2 * g + i // 4][:, cols],
                        rhs=da_codes[(c * GROUPS + g) % 8][:].bitcast(FP8X4),
                        rhs_scale=da_scales[(c * GROUPS + g) % 8][:],
                        start=g == 0,
                        stop=g == GROUPS - 1,
                    )
            nc.vector.scalar_tensor_tensor(
                out=update_view(c, j), in0=grad, scalar=G_INTO_M, in1=moment_view("m", c, j), op0=ALU.mult, op1=ALU.add
            )

        def square_grad(c, j):
            if j % 2 == 0:
                take("work", ("second", c, j // 2))
            nc.scalar.activation(out=second_view(c, j), in_=grad_view(c, j), func=ACT.Square, scale=G_INTO_V)
            give(("grad", c, j))

        def second_moment(c, j):
            view = second_view(c, j)
            nc.vector.tensor_tensor(out=view, in0=view, in1=moment_view("v", c, j), op=ALU.add)

        def inverse_root(c, half):
            second = tile_of(("second", c, half))
            nc.scalar.activation(out=second[:], in_=second[:], func=ACT.Abs_reciprocal_sqrt, scale=V_SCALE)

        def direction(c, j):
            view = update_view(c, j)
            nc.vector.tensor_tensor(out=view, in0=view, in1=second_view(c, j), op=ALU.mult)
            if j % 2 == 1:
                give(("second", c, j // 2))

        def norm_part(c, j):
            take("acc", ("decayed", c, j))
            bank = tile_of(("decayed", c, j))
            for di in range(2):
                for fb in range(2):
                    cols = slice(c * CW + fb * P, c * CW + (fb + 1) * P)
                    nc.tensor.matmul(
                        bank[:, 2 * di + fb, :], lhsT=w1_rows(2 * j + di)[:, cols], rhs=ident_bf[:], start=True, stop=False
                    )
                    nc.tensor.matmul(
                        bank[:, 2 * di + fb, :],
                        lhsT=update_view(c, j)[:, di, fb * P : (fb + 1) * P],
                        rhs=ident[:],
                        is_transpose=True,
                        start=False,
                        stop=True,
                    )
            k = c * PAIRS + j
            nc.scalar.activation(
                out=late["squares"][:],
                in_=bank[:].rearrange("p b r -> p (b r)"),
                func=ACT.Square,
                accum_out=r_sums[:, k : k + 1],
            )
            give(("decayed", c, j))

        def weight_gram():
            take("acc", "gram")
            gram = tile_of("gram")[:, 0, :]
            for i in range(8):
                for fb in range(8):
                    block = w1_rows(i)[:, fb * P : (fb + 1) * P]
                    nc.tensor.matmul(gram, lhsT=block, rhs=block, start=i + fb == 0, stop=i + fb == 14)
            nc.vector.scalar_tensor_tensor(
                out=late["diagonal"][:], in0=gram, scalar=0.25, in1=ident[:], op0=ALU.mult, op1=ALU.mult, accum_out=w_sum[:]
            )
            give("gram")

        def weight_norm():
            take("acc", "w_total")
            total = tile_of("w_total")[:, 0, 0:1]
            nc.tensor.matmul(total, lhsT=ones[:], rhs=w_sum[:], start=True, stop=True)
            nc.vector.reciprocal(out=w_inv[:], in_=total)
            give("w_total")

        def sum_norm_parts():
            nc.vector.tensor_reduce(out=r_sum[:], in_=r_sums[:], axis=mybir.AxisListType.X, op=ALU.add)

        def trust_ratio():
            take("acc", "r_total")
            total = tile_of("r_total")[:, 0, 0:1]
            nc.tensor.matmul(total, lhsT=ones[:], rhs=r_sum[:], start=True, stop=True)
            nc.scalar.activation(out=kappa[:], in_=total, func=ACT.Abs_reciprocal_sqrt, scale=w_inv[:])
            nc.scalar.activation(out=keep_w[:], in_=kappa[:], func=ACT.Identity, scale=-1.0, bias=1.0)
            give("r_total")

        def negate_kappa():
            nc.vector.tensor_scalar(out=minus_kappa[:], in0=kappa[:], scalar1=-1.0, scalar2=None, op0=ALU.mult)

        def final_view(k):
            return tile_of(("final", k))[:].rearrange("p (i f) -> p i f", i=2)

        def decay_weight(k):
            side, j = divmod(k, PAIRS)
            take("work", ("final", k))
            rows = late["w1"][j // 2][:, 2 * (j % 2) : 2 * (j % 2) + 2, side * 512 : (side + 1) * 512]
            nc.scalar.activation(out=final_view(k), in_=rows, func=ACT.Copy, scale=keep_w[:])

        def finish(k):
            side, j = divmod(k, PAIRS)
            view = final_view(k)
            nc.vector.scalar_tensor_tensor(
                out=view, in0=update_tile(2 * side, j), scalar=minus_kappa[:], in1=view, op0=ALU.mult, op1=ALU.add
            )

        def store(k):
            side, j = divmod(k, PAIRS)
            rows = out.rearrange("(i p) f -> p i f", p=P)[:, 2 * j : 2 * j + 2, side * 512 : (side + 1) * 512]
            nc.sync.dma_start(out=rows, in_=final_view(k))

        def step(name, call, args, needs, work_tiles=0, banks=0):
            return (name, call, args, needs, work_tiles, banks)

        def a_load(u):
            return step(("load_a", u), load_a, (u,), [("slope", u - A_TILES, 1)] if u >= A_TILES else [])

        def dy_load(i):
            return step(("load_dy", i), load_dy, (i,), [("turn_dy", i - 4, 1)] if i >= 4 else [])

        def x_load(g):
            return step(("load_x", g), load_x, (g,), [("widen", g - 2)] if g >= 2 else [])

        def moments_load(i):
            c, half = divmod(i, 2)
            needs = [("second", c - 1, 2 * half + 1)] if c else ["late"]
            return step(("load_mv", i), load_moments, (i,), needs)

        sync_queue = [a_load(0), dy_load(0), a_load(1), dy_load(1), a_load(2), a_load(3)]
        sync_queue += [dy_load(i) for i in range(2, 8)]
        sync_queue += [step("load_scales", load_block_scales, (), []), x_load(0), x_load(1), step("load_w2", load_w2, (), [])]
        sync_queue += [a_load(u) for u in range(4, 10)] + [x_load(2), x_load(3), a_load(10), a_load(11)]
        sync_queue += [moments_load(0), moments_load(1)]
        sync_queue += [step(("load_w1", half), load_w1, (half,), ["late"]) for half in range(2)]
        sync_queue += [a_load(u) for u in range(12, 16)] + [moments_load(i) for i in range(2, 8)]
        sync_queue += [step(("store", k), store, (k,), [("finish", k)]) for k in range(2 * PAIRS)]

        def units(c):
            return range(c * GROUPS, (c + 1) * GROUPS)

        def stagger(first, second):
            order = [first[0]]
            for i in range(1, len(first)):
                order.append(first[i])
                if i - 1 < len(second):
                    order.append(second[i - 1])
            return order + second[len(first) - 1 :]

        def read_a(c, names):
            return [step((names[0], u), from_a, (u, names), [("load_a", u)], len(names)) for u in units(c)]

        def densities(c):
            return [step(("pdf", u), density, (u,), [], 1) for u in units(c)]

        def inverses(c, in_place):
            return [step(("inv", u), inverse_abs, (u, in_place), [], 0 if in_place else 1) for u in units(c)]

        def inverse_squares(c):
            return [step(("inv2", u), inverse_square, (u,), []) for u in units(c) if u not in SQUARE_ON_VECTOR]

        def grad_squares(c):
            return [step(("gsq", c, j), square_grad, (c, j), [("first", c, j)], 1 - j % 2) for j in range(PAIRS)]

        def roots(c):
            return [step(("root", c, h), inverse_root, (c, h), [("second", c, 2 * h + 1)]) for h in range(2)]

        def norm_parts(c):
            return [
                step(("norm", c, j), norm_part, (c, j), [("direction", c, j), ("load_w1", j // 2)], 0, 1) for j in range(PAIRS)
            ]

        scalar_queue = stagger(read_a(0, ["square"]), densities(0))
        scalar_queue += stagger(inverses(0, True), inverse_squares(0)) + read_a(0, ["gelu"])
        scalar_queue += read_a(1, ["gelu", "square"]) + densities(1) + stagger(inverses(1, True), inverse_squares(1))
        scalar_queue += stagger(read_a(2, ["square"]), inverses(2, False)) + stagger(inverse_squares(2), grad_squares(0)) + roots(0)
        scalar_queue += [step(("pdf", u), density_in_place, (u,), []) for u in units(2)] + read_a(2, ["gelu"])
        scalar_queue += stagger(read_a(3, ["gelu", "square"]), norm_parts(0)) + stagger(densities(3), grad_squares(1))
        scalar_queue += stagger(inverses(3, True), inverse_squares(3)) + roots(1)
        scalar_queue += grad_squares(2) + roots(2) + norm_parts(1) + grad_squares(3) + norm_parts(2)[:2] + roots(3)
        scalar_queue += norm_parts(2)[2:] + norm_parts(3)
        scalar_queue += [step("trust", trust_ratio, (), ["r_sum", "w_norm"], 0, 1)]
        scalar_queue += [step(("decay", k), decay_weight, (k,), [], 1) for k in range(2 * PAIRS)]

        def dy_steps():
            order = []
            for i in range(2 * GROUPS):
                order.append(step(("turn_dy", i, 0), turn_dy, (i, 0), [("load_dy", i)]))
                if i:
                    order.append(step(("quant_dy", i - 1), quantize_dy, (i - 1,), []))
                order.append(step(("turn_dy", i, 1), turn_dy, (i, 1), []))
            return order

        def widen(g):
            return step(("widen", g), widen_x, (g,), [("load_x", g), "load_scales"])

        def x_steps(g):
            order = [step(("scale_x", g, j), scale_x, (g, j), []) for j in range(8)]
            return order[:5] + [step(("quant_x", g, 0), quantize_x, (g, 0), [])] + order[5:]

        def x_last(g):
            return step(("quant_x", g, 1), quantize_x, (g, 1), [])

        def cdf(u):
            if u in SQUARE_ON_VECTOR:
                return [step(("cdf0", u), cdf_term, (u, False), [("gelu", u), ("inv", u)])]
            return []

        def cdf_last(u):
            made = ("inv", u) if u in SQUARE_ON_VECTOR else ("inv2", u)
            return [step(("cdf", u), cdf_term, (u, True), [("gelu", u), made])]

        def slopes(u):
            return [step(("slope", u, fb), make_slope, (u, fb), [("pdf", u)]) for fb in range(2)]

        def das(u):
            return [step(("da", u, fb), make_da, (u, fb), ["load_w2"]) for fb in range(2)]

        def quant(u):
            return [step(("quant_da", u), quantize_da, (u,), [])]

        def first(c, j, after=()):
            needs = [("load_mv", 2 * c + j // 2)] + list(after)
            return [step(("first", c, j), first_moment, (c, j), needs, 1 if c == 2 else 0, 1)]

        def second(c, j):
            return [step(("second", c, j), second_moment, (c, j), [("gsq", c, j)])]

        def directions(c):
            return [step(("direction", c, j), direction, (c, j), [("root", c, j // 2)]) for j in range(PAIRS)]

        def chain(u, extra):
            ahead = cdf(u + 1) if u + 1 < UNITS else []
            ahead_last = cdf_last(u + 1) if u + 1 < UNITS else []
            behind = quant(u - 1) if u else []
            return slopes(u)[:1] + behind + slopes(u)[1:] + ahead + das(u)[:1] + ahead_last + das(u)[1:] + extra

        vector_queue = dy_steps() + [widen(0), step(("quant_dy", 7), quantize_dy, (7,), [])] + x_steps(0)
        vector_queue += [widen(1), x_last(0)] + x_steps(1) + [widen(2), x_last(1)] + cdf(0) + x_steps(2)[:2] + cdf_last(0) + x_steps(2)[2:]
        vector_queue += chain(0, [widen(3), x_last(2)]) + chain(1, x_steps(3)) + chain(2, [x_last(3)]) + chain(3, [])
        vector_queue += chain(4, first(0, 0) + first(0, 1))
        vector_queue += chain(5, first(0, 2) + second(0, 0) + first(0, 3) + second(0, 1) + second(0, 2) + second(0, 3))
        vector_queue += chain(6, [step("gram", weight_gram, (), [("load_w1", 0), ("load_w1", 1)], 0, 1)] + directions(0))
        vector_queue += chain(7, [step("w_norm", weight_norm, (), [], 0, 1)])
        vector_queue += chain(8, first(1, 0, [("norm", 0, 3)]) + first(1, 1)) + chain(9, first(1, 2) + second(1, 0) + first(1, 3) + second(1, 1))
        vector_queue += chain(10, second(1, 2) + second(1, 3)) + chain(11, [])
        vector_queue += chain(12, first(2, 0) + first(2, 1)) + chain(13, first(2, 2) + second(2, 0) + first(2, 3) + second(2, 1))
        vector_queue += chain(14, second(2, 2) + second(2, 3) + directions(1)) + chain(15, directions(2)[:2]) + quant(15)
        vector_queue += directions(2)[2:] + first(3, 0, [("norm", 1, 3)]) + first(3, 1) + second(3, 0) + first(3, 2) + second(3, 1) + first(3, 3)
        vector_queue += second(3, 2) + second(3, 3) + directions(3)
        vector_queue += [step("r_sum", sum_norm_parts, (), [("norm", c, j) for c in range(CHUNKS) for j in range(PAIRS)])]
        vector_queue += [step("negate", negate_kappa, (), ["trust"])]
        vector_queue += [step(("finish", k), finish, (k,), [("decay", k)]) for k in range(2 * PAIRS)]

        queues = [sync_queue, scalar_queue, vector_queue]
        position = [0, 0, 0]
        done = set()

        def emit(until):
            moved = True
            while moved and until not in done:
                moved = False
                for q in range(3):
                    ready = True
                    while ready and position[q] < len(queues[q]) and until not in done:
                        name, call, args, needs, work_tiles, banks = queues[q][position[q]]
                        ready = (
                            all(need in done for need in needs)
                            and len(free["work"]) >= work_tiles
                            and len(free["acc"]) >= banks
                        )
                        if ready:
                            call(*args)
                            done.add(name)
                            position[q] = position[q] + 1
                            moved = True
            assert until in done, [queues[q][min(position[q], len(queues[q]) - 1)][0] for q in range(3)]

        with tc.tile_pool(name="head", bufs=1) as head:
            late["dy_raw"] = [head.tile([P, 2, D], BF16, name="dy_raw%d" % i) for i in range(4)]
            late["dy_t"] = [head.tile([P, 2, 2, P, 2], F32, name="dy_t%d" % i, align_bytes=64) for i in range(2)]
            late["x_raw"] = [head.tile([P, PACK * D], U8, name="x_raw%d" % i) for i in range(2)]
            late["x_wide"] = head.tile([P, PACK, D], BF16, name="x_wide")
            late["x_packed"] = [head.tile([P, D // 2, PACK], BF16, name="x_packed%d" % i, align_bytes=64) for i in range(2)]
            emit(("quant_x", GROUPS - 1, 1))
        with tc.tile_pool(name="tail", bufs=1) as tail:
            late["m"] = [tail.tile([P, 4, CW], BF16, name="m_tile%d" % i) for i in range(2)]
            late["v"] = [tail.tile([P, 4, CW], BF16, name="v_tile%d" % i) for i in range(2)]
            late["w1"] = [tail.tile([P, 4, F], BF16, name="w1_tile%d" % i) for i in range(2)]
            late["update"] = [tail.tile([P, 2, 2 * CW], F32, name="update%d" % i) for i in range(PAIRS)]
            late["squares"] = tail.tile([P, 512], F32, name="squares")
            late["diagonal"] = tail.tile([P, P], F32, name="diagonal")
            done.add("late")
            emit(("store", 2 * PAIRS - 1))
